import numpy as np
import ml_dtypes

BF16 = ml_dtypes.bfloat16


def bf(x):
    return np.asarray(x, np.float32).astype(BF16)


def f32(x):
    return np.asarray(x, np.float32)


def f64(x):
    return np.asarray(x).astype(np.float64)


def striped(idx):
    return np.tile(idx.reshape(-1, 16).T, (8, 1))


A, S, K, M, N, E, Q = 256, 512, 512, 256, 256, 2, 128


def setup_inputs():
    return {"a": bf(np.random.standard_normal((A, S))), "wd": bf(np.random.standard_normal((A, M)) / np.sqrt(A)), "x": bf(np.random.standard_normal((K, N))), "w": bf(1.2 * np.random.standard_normal((E, K, M)) / np.sqrt(K)), "s": f32(0.5 + np.random.random_sample((M, 1))), "offs": striped(np.random.permutation(S)[:N])}


def reference(a, wd, x, w, s, offs):
    idx = offs[:16].T.reshape(-1)
    z = f64(wd).T @ f64(a)
    for e in range(E):
        z[:, idx[e * Q : (e + 1) * Q]] += f64(w)[e].T @ f64(x)[:, e * Q : (e + 1) * Q]
    z = z / np.sqrt((z**2).mean(axis=0, keepdims=True) + 1e-5) * f64(s)
    return z

@@ -1,0 +1,82 @@
+import concourse.mybir as mybir
+
+BF16, F32, U16 = mybir.dt.bfloat16, mybir.dt.float32, mybir.dt.uint16
+ACT = mybir.ActivationFunctionType
+MULT = mybir.AluOpType.mult
+
+A, S, K, M, N, E, Q = 256, 512, 512, 256, 256, 2, 128
+P = 128
+EPS = 1e-5
+
+FLOPS = 2 * A * M * S + 2 * K * M * N + 2 * M * S
+
+
+def tile_rows_placenorm_proj_kernel(tc, a, wd, x, w, s, offs, out):
+    nc = tc.nc
+    a_blocks, k_blocks, windows = A // P, K // P, M // P
+    piece_columns = Q // 16
+
+    with (
+        tc.tile_pool(name="held", bufs=1) as held,
+        tc.psum_pool(name="psum", bufs=1) as psum,
+    ):
+        a_tile = held.tile([P, a_blocks, S], BF16)
+        wd_tile = held.tile([P, a_blocks, M], BF16)
+        offsets = held.tile([P, N // 16], U16)
+        x_tile = held.tile([P, k_blocks, N], BF16)
+        w_tiles = [held.tile([P, k_blocks, M], BF16, name=f"w{e}") for e in range(E)]
+        gain = held.tile([P, windows], F32)
+
+        nc.sync.dma_start(wd_tile[:], wd.rearrange("(p c) m -> p c m", p=P))
+        nc.sync.dma_start(a_tile[:], a.rearrange("(p c) i -> p c i", p=P))
+        nc.sync.dma_start(offsets[:], offs)
+        nc.sync.dma_start(x_tile[:], x.rearrange("(p c) j -> p c j", p=P))
+        for e in range(E):
+            nc.sync.dma_start(w_tiles[e][:], w[e].rearrange("(p c) m -> p c m", p=P))
+        nc.sync.dma_start(gain[:], s.rearrange("(v p) o -> p (v o)", p=P))
+
+        mean_weights = held.tile([P, P], BF16)
+        nc.vector.memset(mean_weights[:], 1.0 / M)
+        eps = held.tile([P, 1], F32)
+        nc.vector.memset(eps[:], EPS)
+
+        z = [psum.tile([P, S], F32, name=f"z{v}") for v in range(windows)]
+        for v in range(windows):
+            for c in range(a_blocks):
+                nc.tensor.matmul(
+                    z[v][:],
+                    wd_tile[:, c, v * P : (v + 1) * P],
+                    a_tile[:, c, :],
+                    start=c == 0,
+                    stop=False,
+                )
+
+        for e in range(E):
+            piece = offsets[:, e * piece_columns : (e + 1) * piece_columns]
+            for v in range(windows):
+                for c in range(k_blocks):
+                    nc.tensor.matmul(
+                        z[v][:].indirect(piece),
+                        w_tiles[e][:, c, v * P : (v + 1) * P],
+                        x_tile[:, c, e * Q : (e + 1) * Q],
+                        start=False,
+                        stop=e == E - 1 and c == k_blocks - 1,
+                    )
+
+        mean = psum.tile([P, S], F32)
+        squares = [held.tile([P, S], BF16, name=f"squares{v}") for v in range(windows)]
+        for v in range(windows):
+            nc.scalar.activation(squares[v][:], z[v][:], ACT.Square)
+        for v in reversed(range(windows)):
+            nc.tensor.matmul(
+                mean[:], mean_weights[:], squares[v][:], start=v == windows - 1, stop=v == 0
+            )
+        rstd = held.tile([P, S], F32)
+        nc.scalar.activation(rstd[:], mean[:], ACT.Abs_reciprocal_sqrt, bias=eps[:])
+
+        for v in range(windows):
+            result = held.tile([P, S], F32, name=f"result{v}")
+            nc.vector.scalar_tensor_tensor(
+                result[:], z[v][:], gain[:, v : v + 1], rstd[:], MULT, MULT
+            )
+            nc.sync.dma_start(out[v * P : (v + 1) * P, :], result[:])

@@ -7,6 +7,7 @@ MULT = mybir.AluOpType.mult
 A, S, K, M, N, E, Q = 256, 512, 512, 256, 256, 2, 128
 P = 128
 EPS = 1e-5
+WARM_MATMULS = 4
 
 FLOPS = 2 * A * M * S + 2 * K * M * N + 2 * M * S
 
@@ -39,6 +40,14 @@ def tile_rows_placenorm_proj_kernel(tc, a, wd, x, w, s, offs, out):
         nc.vector.memset(mean_weights[:], 1.0 / M)
         eps = held.tile([P, 1], F32)
         nc.vector.memset(eps[:], EPS)
+        warm_rstd = held.tile([P, 1], F32)
+        nc.scalar.activation(warm_rstd[:], eps[:], ACT.Abs_reciprocal_sqrt, bias=eps[:])
+
+        zeros = held.tile([P, S], BF16)
+        nc.vector.memset(zeros[:], 0.0)
+        warm_bank = psum.tile([P, S], F32)
+        for i in range(WARM_MATMULS):
+            nc.tensor.matmul(warm_bank[:], zeros[:, :P], zeros[:], start=True, stop=True)
 
         z = [psum.tile([P, S], F32, name=f"z{v}") for v in range(windows)]
         for v in range(windows):

@@ -7,6 +7,7 @@ MULT = mybir.AluOpType.mult
 A, S, K, M, N, E, Q = 256, 512, 512, 256, 256, 2, 128
 P = 128
 EPS = 1e-5
+HALF = S // 2
 WARM_MATMULS = 4
 
 FLOPS = 2 * A * M * S + 2 * K * M * N + 2 * M * S
@@ -36,15 +37,15 @@ def tile_rows_placenorm_proj_kernel(tc, a, wd, x, w, s, offs, out):
             nc.sync.dma_start(w_tiles[e][:], w[e].rearrange("(p c) m -> p c m", p=P))
         nc.sync.dma_start(gain[:], s.rearrange("(v p) o -> p (v o)", p=P))
 
+        zeros = held.tile([P, S], BF16)
+        nc.vector.memset(zeros[:], 0.0)
         mean_weights = held.tile([P, P], BF16)
-        nc.vector.memset(mean_weights[:], 1.0 / M)
+        nc.gpsimd.memset(mean_weights[:], 1.0 / M)
         eps = held.tile([P, 1], F32)
-        nc.vector.memset(eps[:], EPS)
+        nc.gpsimd.memset(eps[:], EPS)
         warm_rstd = held.tile([P, 1], F32)
         nc.scalar.activation(warm_rstd[:], eps[:], ACT.Abs_reciprocal_sqrt, bias=eps[:])
 
-        zeros = held.tile([P, S], BF16)
-        nc.vector.memset(zeros[:], 0.0)
         warm_bank = psum.tile([P, S], F32)
         for i in range(WARM_MATMULS):
             nc.tensor.matmul(warm_bank[:], zeros[:, :P], zeros[:], start=True, stop=True)
@@ -72,20 +73,27 @@ def tile_rows_placenorm_proj_kernel(tc, a, wd, x, w, s, offs, out):
                         stop=e == E - 1 and c == k_blocks - 1,
                     )
 
-        mean = psum.tile([P, S], F32)
+        halves = [slice(h * HALF, (h + 1) * HALF) for h in range(S // HALF)]
         squares = [held.tile([P, S], BF16, name=f"squares{v}") for v in range(windows)]
-        for v in range(windows):
+        mean = [psum.tile([P, HALF], F32, name=f"mean{h}") for h in range(len(halves))]
+        rstd = [held.tile([P, HALF], F32, name=f"rstd{h}") for h in range(len(halves))]
+        for v in range(windows - 1):
             nc.scalar.activation(squares[v][:], z[v][:], ACT.Square)
-        for v in reversed(range(windows)):
-            nc.tensor.matmul(
-                mean[:], mean_weights[:], squares[v][:], start=v == windows - 1, stop=v == 0
-            )
-        rstd = held.tile([P, S], F32)
-        nc.scalar.activation(rstd[:], mean[:], ACT.Abs_reciprocal_sqrt, bias=eps[:])
-
-        for v in range(windows):
-            result = held.tile([P, S], F32, name=f"result{v}")
-            nc.vector.scalar_tensor_tensor(
-                result[:], z[v][:], gain[:, v : v + 1], rstd[:], MULT, MULT
-            )
-            nc.sync.dma_start(out[v * P : (v + 1) * P, :], result[:])
+        for columns in halves:
+            nc.scalar.activation(squares[windows - 1][:, columns], z[windows - 1][:, columns], ACT.Square)
+        for h, columns in enumerate(halves):
+            for v in range(windows):
+                nc.tensor.matmul(
+                    mean[h][:],
+                    mean_weights[:],
+                    squares[v][:, columns],
+                    start=v == 0,
+                    stop=v == windows - 1,
+                )
+            nc.scalar.activation(rstd[h][:], mean[h][:], ACT.Abs_reciprocal_sqrt, bias=eps[:])
+            for v in range(windows):
+                result = held.tile([P, HALF], F32, name=f"result{v}{h}")
+                nc.vector.scalar_tensor_tensor(
+                    result[:], z[v][:, columns], gain[:, v : v + 1], rstd[h][:], MULT, MULT
+                )
+                nc.sync.dma_start(out[v * P : (v + 1) * P, columns], result[:])

@@ -8,7 +8,7 @@ A, S, K, M, N, E, Q = 256, 512, 512, 256, 256, 2, 128
 P = 128
 EPS = 1e-5
 HALF = S // 2
-WARM_MATMULS = 4
+WARM_MATMULS = 3
 
 FLOPS = 2 * A * M * S + 2 * K * M * N + 2 * M * S
 
@@ -30,7 +30,9 @@ def tile_rows_placenorm_proj_kernel(tc, a, wd, x, w, s, offs, out):
         gain = held.tile([P, windows], F32)
 
         nc.sync.dma_start(wd_tile[:], wd.rearrange("(p c) m -> p c m", p=P))
-        nc.sync.dma_start(a_tile[:], a.rearrange("(p c) i -> p c i", p=P))
+        a_blocks_dram = a.rearrange("(p c) i -> p c i", p=P)
+        for c in range(a_blocks):
+            nc.sync.dma_start(a_tile[:, c, :], a_blocks_dram[:, c, :])
         nc.sync.dma_start(offsets[:], offs)
         nc.sync.dma_start(x_tile[:], x.rearrange("(p c) j -> p c j", p=P))
         for e in range(E):
@@ -51,8 +53,8 @@ def tile_rows_placenorm_proj_kernel(tc, a, wd, x, w, s, offs, out):
             nc.tensor.matmul(warm_bank[:], zeros[:, :P], zeros[:], start=True, stop=True)
 
         z = [psum.tile([P, S], F32, name=f"z{v}") for v in range(windows)]
-        for v in range(windows):
-            for c in range(a_blocks):
+        for c in range(a_blocks):
+            for v in range(windows):
                 nc.tensor.matmul(
                     z[v][:],
                     wd_tile[:, c, v * P : (v + 1) * P],

import concourse.mybir as mybir

BF16, F32, U16 = mybir.dt.bfloat16, mybir.dt.float32, mybir.dt.uint16
ACT = mybir.ActivationFunctionType
MULT = mybir.AluOpType.mult

A, S, K, M, N, E, Q = 256, 512, 512, 256, 256, 2, 128
P = 128
EPS = 1e-5
HALF = S // 2
WARM_MATMULS = 3

FLOPS = 2 * A * M * S + 2 * K * M * N + 2 * M * S


def tile_rows_placenorm_proj_kernel(tc, a, wd, x, w, s, offs, out):
    nc = tc.nc
    a_blocks, k_blocks, windows = A // P, K // P, M // P
    piece_columns = Q // 16

    with (
        tc.tile_pool(name="held", bufs=1) as held,
        tc.psum_pool(name="psum", bufs=1) as psum,
    ):
        a_tile = held.tile([P, a_blocks, S], BF16)
        wd_tile = held.tile([P, a_blocks, M], BF16)
        offsets = held.tile([P, N // 16], U16)
        x_tile = held.tile([P, k_blocks, N], BF16)
        w_tiles = [held.tile([P, k_blocks, M], BF16, name=f"w{e}") for e in range(E)]
        gain = held.tile([P, windows], F32)

        nc.sync.dma_start(wd_tile[:], wd.rearrange("(p c) m -> p c m", p=P))
        a_blocks_dram = a.rearrange("(p c) i -> p c i", p=P)
        for c in range(a_blocks):
            nc.sync.dma_start(a_tile[:, c, :], a_blocks_dram[:, c, :])
        nc.sync.dma_start(offsets[:], offs)
        nc.sync.dma_start(x_tile[:], x.rearrange("(p c) j -> p c j", p=P))
        for e in range(E):
            nc.sync.dma_start(w_tiles[e][:], w[e].rearrange("(p c) m -> p c m", p=P))
        nc.sync.dma_start(gain[:], s.rearrange("(v p) o -> p (v o)", p=P))

        zeros = held.tile([P, S], BF16)
        nc.vector.memset(zeros[:], 0.0)
        mean_weights = held.tile([P, P], BF16)
        nc.gpsimd.memset(mean_weights[:], 1.0 / M)
        eps = held.tile([P, 1], F32)
        nc.gpsimd.memset(eps[:], EPS)
        warm_rstd = held.tile([P, 1], F32)
        nc.scalar.activation(warm_rstd[:], eps[:], ACT.Abs_reciprocal_sqrt, bias=eps[:])

        warm_bank = psum.tile([P, S], F32)
        for i in range(WARM_MATMULS):
            nc.tensor.matmul(warm_bank[:], zeros[:, :P], zeros[:], start=True, stop=True)

        z = [psum.tile([P, S], F32, name=f"z{v}") for v in range(windows)]
        for c in range(a_blocks):
            for v in range(windows):
                nc.tensor.matmul(
                    z[v][:],
                    wd_tile[:, c, v * P : (v + 1) * P],
                    a_tile[:, c, :],
                    start=c == 0,
                    stop=False,
                )

        for e in range(E):
            piece = offsets[:, e * piece_columns : (e + 1) * piece_columns]
            for v in range(windows):
                for c in range(k_blocks):
                    nc.tensor.matmul(
                        z[v][:].indirect(piece),
                        w_tiles[e][:, c, v * P : (v + 1) * P],
                        x_tile[:, c, e * Q : (e + 1) * Q],
                        start=False,
                        stop=e == E - 1 and c == k_blocks - 1,
                    )

        halves = [slice(h * HALF, (h + 1) * HALF) for h in range(S // HALF)]
        squares = [held.tile([P, S], BF16, name=f"squares{v}") for v in range(windows)]
        mean = [psum.tile([P, HALF], F32, name=f"mean{h}") for h in range(len(halves))]
        rstd = [held.tile([P, HALF], F32, name=f"rstd{h}") for h in range(len(halves))]
        for v in range(windows - 1):
            nc.scalar.activation(squares[v][:], z[v][:], ACT.Square)
        for columns in halves:
            nc.scalar.activation(squares[windows - 1][:, columns], z[windows - 1][:, columns], ACT.Square)
        for h, columns in enumerate(halves):
            for v in range(windows):
                nc.tensor.matmul(
                    mean[h][:],
                    mean_weights[:],
                    squares[v][:, columns],
                    start=v == 0,
                    stop=v == windows - 1,
                )
            nc.scalar.activation(rstd[h][:], mean[h][:], ACT.Abs_reciprocal_sqrt, bias=eps[:])
            for v in range(windows):
                result = held.tile([P, HALF], F32, name=f"result{v}{h}")
                nc.vector.scalar_tensor_tensor(
                    result[:], z[v][:, columns], gain[:, v : v + 1], rstd[h][:], MULT, MULT
                )
                nc.sync.dma_start(out[v * P : (v + 1) * P, columns], result[:])
